import numpy as np
import ml_dtypes


def mxq(x, axis, fmt="e4m3"):
    dtype, down = {"e4m3": (ml_dtypes.float8_e4m3fn, 7), "e5m2": (ml_dtypes.float8_e5m2, 14)}[fmt]
    v = np.moveaxis(np.asarray(x, np.float32).astype(ml_dtypes.bfloat16).astype(np.float64), axis, -1)
    blocks = v.reshape(v.shape[:-1] + (-1, 32))
    amax = np.abs(blocks).max(-1, keepdims=True)
    byte = np.maximum(np.where(amax > 0, np.frexp(amax)[1] - 1 + 127, 0) - down, 1)
    scale = np.exp2(byte - 127.0)
    codes = (blocks / scale).astype(np.float32).astype(dtype).astype(np.float64)
    return np.moveaxis((codes * scale).reshape(v.shape), -1, axis)


WIDE = False


def mx_kscale(k):
    if not WIDE:
        return np.ones(k)
    levels = np.array([10, -10, 5, -5, 0])
    if k % 512:
        return np.exp2(np.random.permutation(np.resize(levels, k // 32))).repeat(32)
    a = np.empty((k // 512, 16))
    for p in range(k // 512):
        a[p, :8] = np.random.permutation(np.resize(levels, 8))
        for g in range(8):
            far = levels[np.abs(levels - a[p, g]) >= 10]
            a[p, g + 8] = far[np.random.randint(len(far))]
    return np.exp2(a.ravel()).repeat(32)


def f64(x):
    return np.asarray(x).astype(np.float64)


def striped(idx):
    return np.tile(idx.reshape(-1, 16).T, (8, 1)).astype(np.uint16)


def unstriped(offs):
    return offs[:16].T.reshape(-1).astype(np.int64)


def relu(v):
    return np.maximum(v, 0.0)


K, T, D, S, V, N = 2048, 512, 4, 1024, 256, 512


def setup_inputs():
    n = np.random.standard_normal
    s = mx_kscale(K)[:, None]
    return {
        "xT": (n((K, T)) * s).astype(np.float32),
        "w": (n((K, N)) / np.sqrt(K) / s).astype(np.float32),
        "b": (0.3 * n((N, 1))).astype(np.float32),
        "gate": np.tile(np.random.uniform(0.2, 1.0, (D, 1, V)) / np.sqrt(D), (1, N, 1)).astype(np.float32),
        "pos1": striped(np.random.permutation(T)[:V]),
        "pos2": striped(np.random.permutation(T)[:V]),
        "pos3": striped(np.random.permutation(T)[:V]),
        "pos4": striped(np.random.permutation(T)[:V]),
    }


def reference(xT, w, b, gate, pos1, pos2, pos3, pos4):
    y = mxq(f64(w), 0, "e4m3").T @ mxq(f64(xT), 0, "e4m3")
    y = relu(y + f64(b))
    return sum(f64(gate[d]) * y[:, unstriped(p)] for d, p in enumerate((pos1, pos2, pos3, pos4)))

@@ -1,0 +1,198 @@
+from contextlib import ExitStack
+
+import concourse.mybir as mybir
+
+K, T, D, V, N = 2048, 512, 4, 256, 512
+FLOPS = 2 * K * T * N + 2 * D * N * V
+
+F32 = mybir.dt.float32
+BF16 = mybir.dt.bfloat16
+U32 = mybir.dt.uint32
+U16 = mybir.dt.uint16
+U8 = mybir.dt.uint8
+FP8X4 = mybir.dt.float8_e4m3fn_x4
+ADD, MULT = mybir.AluOpType.add, mybir.AluOpType.mult
+COPY, RELU = mybir.ActivationFunctionType.Copy, mybir.ActivationFunctionType.Relu
+
+P = 128
+PACK = 4
+K_PASS = P * PACK
+PASSES = K // K_PASS
+HALF = 256
+V_NODES = 320
+
+
+def interleave(engine_copy, dst, src):
+    engine_copy(
+        dst.rearrange("p (c i) t -> p c t i", i=4),
+        src.rearrange("p t (c i) -> p c t i", i=4),
+    )
+
+
+def tile_picked_agg_lin_relu_sub_l_kernel(
+    tc, xT, w, b, gate, pos1, pos2, pos3, pos4, out
+):
+    nc = tc.nc
+    lists = (pos1, pos2, pos3, pos4)
+
+    def v_copy(dst, src):
+        nc.vector.tensor_copy(out=dst, in_=src)
+
+    def s_copy(dst, src):
+        nc.scalar.copy(out=dst, in_=src)
+
+    with ExitStack() as ctx:
+        keep = ctx.enter_context(tc.tile_pool(name="keep", bufs=1))
+        psum = ctx.enter_context(tc.psum_pool(name="psum", bufs=1))
+
+        offs = [keep.tile([P, V // 16], U16, name=f"offs{d}") for d in range(D)]
+        bias = keep.tile([P, 2, 2], F32, name="bias")
+        warm = keep.tile([P, 1], F32, name="warm")
+        w_raw = [[keep.tile([P, PACK, HALF], F32, name=f"wr{h}{c}") for c in range(PASSES)] for h in range(2)]
+        w_bf = [[keep.tile([P, HALF, PACK], BF16, name=f"wb{h}{c}", align_bytes=64) for c in range(PASSES)] for h in range(2)]
+        w_q = [[keep.tile([P, HALF], U32, name=f"wq{h}{c}", align_bytes=64) for c in range(PASSES)] for h in range(2)]
+        w_s = [[keep.tile([P, HALF], U8, name=f"ws{h}{c}", align_bytes=64) for c in range(PASSES)] for h in range(2)]
+        x_raw = [keep.tile([P, PACK, T], F32, name=f"xr{c}") for c in range(PASSES - 1)]
+        x_last = [keep.tile([P, PACK, T // 2], F32, name=f"xl{t}") for t in range(2)]
+        x_bf = [keep.tile([P, T, PACK], BF16, name=f"xb{c}", align_bytes=64) for c in range(PASSES)]
+        x_q = [keep.tile([P, T], U32, name=f"xq{c}", align_bytes=64) for c in range(PASSES)]
+        x_s = [keep.tile([P, T], U8, name=f"xs{c}", align_bytes=64) for c in range(PASSES)]
+        g_sb = [[keep.tile([P, 2, 2, V], F32, name=f"g{h}{dd}") for dd in range(2)] for h in range(2)]
+        y = [keep.tile([P, T], F32, name=f"y{m}") for m in range(4)]
+        prod = [[keep.tile([P, 2, V], F32, name=f"pr{h}{d}") for d in range(D)] for h in range(2)]
+        part = [[keep.tile([P, 2, V], F32, name=f"pa{h}{i}") for i in range(2)] for h in range(2)]
+        res = [[keep.tile([P, V], F32, name=f"res{h}{e}") for e in range(2)] for h in range(2)]
+
+        nc.scalar.dma_start(out=bias[:], in_=b.rearrange("(h p e) o -> p h (e o)", h=2, e=2))
+
+        def load_w(h):
+            for c in range(PASSES):
+                src = w[c * K_PASS : (c + 1) * K_PASS, h * HALF : (h + 1) * HALF]
+                nc.sync.dma_start(out=w_raw[h][c][:], in_=src.rearrange("(p j) n -> p j n", j=PACK))
+
+        def load_g(h):
+            for dd in range(2):
+                src = gate[2 * dd : 2 * dd + 2, h * HALF : (h + 1) * HALF, :]
+                nc.sync.dma_start(
+                    out=g_sb[h][dd][:].rearrange("p d e v -> p d (e v)"),
+                    in_=src.rearrange("d (p e) v -> p d (e v)", e=2),
+                )
+
+        load_w(0)
+        for c in range(PASSES - 1):
+            src = xT[c * K_PASS : (c + 1) * K_PASS, :]
+            nc.sync.dma_start(out=x_raw[c][:], in_=src.rearrange("(p j) n -> p j n", j=PACK))
+            if c == 1:
+                for d in range(D):
+                    nc.sync.dma_start(offs[d][:], lists[d])
+        for t in range(2):
+            src = xT[(PASSES - 1) * K_PASS :, t * (T // 2) : (t + 1) * (T // 2)]
+            nc.sync.dma_start(out=x_last[t][:], in_=src.rearrange("(p j) n -> p j n", j=PACK))
+        load_g(0)
+        load_w(1)
+        load_g(1)
+
+        def interleave_w(h, c):
+            s_copy(
+                w_bf[h][c][:].rearrange("p (e m) j -> p e m j", e=2),
+                w_raw[h][c][:].rearrange("p j (m e) -> p e m j", e=2),
+            )
+
+        def quantise_w(h, c):
+            nc.vector.quantize_mx(
+                out=w_q[h][c][:].bitcast(FP8X4),
+                scales=w_s[h][c][:],
+                in_=w_bf[h][c][:].rearrange("p n j -> p (n j)"),
+            )
+
+        def quantise_x(c, a, z):
+            nc.vector.quantize_mx(
+                out=x_q[c][:, a:z].bitcast(FP8X4),
+                scales=x_s[c][:, a:z],
+                in_=x_bf[c][:, a:z, :].rearrange("p n j -> p (n j)"),
+            )
+
+        def multiply(bank, h, e, c, a, z):
+            cols = slice(e * P, (e + 1) * P)
+            nc.tensor.matmul_mx(
+                out=bank[:],
+                lhsT=w_q[h][c][:, cols].bitcast(FP8X4),
+                lhsT_scale=w_s[h][c][:, cols],
+                rhs=x_q[c][:, a:z].bitcast(FP8X4),
+                rhs_scale=x_s[c][:, a:z],
+                start=(c == 0),
+                stop=(c == PASSES - 1),
+            )
+
+        def activate(bank, h, e, a, z):
+            nc.scalar.activation(
+                out=y[2 * h + e][:, a:z], in_=bank[:], func=RELU, bias=bias[:, h, e : e + 1], scale=1.0
+            )
+
+        def gather(h, d, e):
+            nc.vector.tensor_tensor(
+                prod[h][d][:, e, :],
+                y[2 * h + e][:].indirect(offs[d][:]),
+                g_sb[h][d // 2][:, d % 2, e, :],
+                MULT,
+            )
+
+        def add(dst, one, two):
+            nc.vector.tensor_tensor(dst, one, two, ADD)
+
+        def finish(h, e):
+            add(res[h][e][:], part[h][1][:, e, :], prod[h][3][:, e, :])
+            dst = out[h * HALF : (h + 1) * HALF, :].rearrange("(p e) v -> p e v", e=2)
+            nc.sync.dma_start(out=dst[:, e, :], in_=res[h][e][:])
+
+        def second_half(c):
+            interleave_w(1, c)
+            quantise_w(1, c)
+            for e in range(2):
+                multiply(banks1[e], 1, e, c, 0, T)
+
+        nc.vector.memset(warm[:], 0.0)
+        nc.scalar.activation(out=warm[:], in_=warm[:], func=RELU)
+
+        banks0 = [[psum.tile([P, T // 2], F32, name=f"b0{e}{t}") for t in range(2)] for e in range(2)]
+        banks1 = [psum.tile([P, T], F32, name=f"b1{e}") for e in range(2)]
+
+        for c in range(PASSES):
+            interleave_w(0, c)
+            quantise_w(0, c)
+        for c in range(PASSES - 1):
+            interleave(v_copy, x_bf[c][:, :V_NODES, :], x_raw[c][:, :, :V_NODES])
+            interleave(s_copy, x_bf[c][:, V_NODES:, :], x_raw[c][:, :, V_NODES:])
+            quantise_x(c, 0, T)
+            for e in range(2):
+                for t in range(2):
+                    multiply(banks0[e][t], 0, e, c, t * (T // 2), (t + 1) * (T // 2))
+        for t in range(2):
+            a, z = t * (T // 2), (t + 1) * (T // 2)
+            cut = 160
+            interleave(v_copy, x_bf[PASSES - 1][:, a : a + cut, :], x_last[t][:, :, :cut])
+            interleave(s_copy, x_bf[PASSES - 1][:, a + cut : z, :], x_last[t][:, :, cut:])
+            quantise_x(PASSES - 1, a, z)
+            for e in range(2):
+                multiply(banks0[e][t], 0, e, PASSES - 1, a, z)
+            for e in range(2):
+                activate(banks0[e][t], 0, e, a, z)
+
+        def aggregate(h, between):
+            for d in range(D):
+                gather(h, d, 0)
+                if d == 2:
+                    add(part[h][0][:], prod[h][0][:], prod[h][1][:])
+                if d == 3:
+                    add(part[h][1][:], part[h][0][:], prod[h][2][:])
+                between(d)
+                gather(h, d, 1)
+            for e in range(2):
+                finish(h, e)
+
+        aggregate(0, lambda d: second_half(d - 2) if d >= 2 else None)
+        second_half(2)
+        second_half(3)
+        for e in range(2):
+            activate(banks1[e], 1, e, 0, T)
+        aggregate(1, lambda d: None)

@@ -1,6 +1,7 @@
 from contextlib import ExitStack
 
 import concourse.mybir as mybir
+from concourse.masks import make_identity
 
 K, T, D, V, N = 2048, 512, 4, 256, 512
 FLOPS = 2 * K * T * N + 2 * D * N * V
@@ -12,187 +13,216 @@ U16 = mybir.dt.uint16
 U8 = mybir.dt.uint8
 FP8X4 = mybir.dt.float8_e4m3fn_x4
 ADD, MULT = mybir.AluOpType.add, mybir.AluOpType.mult
-COPY, RELU = mybir.ActivationFunctionType.Copy, mybir.ActivationFunctionType.Relu
+RELU = mybir.ActivationFunctionType.Relu
 
 P = 128
 PACK = 4
 K_PASS = P * PACK
 PASSES = K // K_PASS
-HALF = 256
+LAST = PASSES - 1
+BLOCKS = N // P
+W_COLS = ((0, P), (P, 2 * P), (2 * P, N))
+GROUP = (0, 1, 2, 2)
+
+RANGES = (((0, 256), (256, 384), (384, T)), ((0, T),), ((0, T),), ((0, T),))
+
 V_NODES = 320
-
-
-def interleave(engine_copy, dst, src):
-    engine_copy(
-        dst.rearrange("p (c i) t -> p c t i", i=4),
-        src.rearrange("p t (c i) -> p c t i", i=4),
-    )
+LAST_LOADS = ((0, 240, 384), (384, 464, T))
 
 
 def tile_picked_agg_lin_relu_sub_l_kernel(
     tc, xT, w, b, gate, pos1, pos2, pos3, pos4, out
 ):
     nc = tc.nc
-    lists = (pos1, pos2, pos3, pos4)
-
-    def v_copy(dst, src):
-        nc.vector.tensor_copy(out=dst, in_=src)
-
-    def s_copy(dst, src):
-        nc.scalar.copy(out=dst, in_=src)
 
     with ExitStack() as ctx:
         keep = ctx.enter_context(tc.tile_pool(name="keep", bufs=1))
+        turns = ctx.enter_context(tc.tile_pool(name="turns", bufs=1))
         psum = ctx.enter_context(tc.psum_pool(name="psum", bufs=1))
 
         offs = [keep.tile([P, V // 16], U16, name=f"offs{d}") for d in range(D)]
-        bias = keep.tile([P, 2, 2], F32, name="bias")
+        bias_rows = keep.tile([P, P], F32, name="bias_rows")
+        ident = keep.tile([P, P], F32, name="ident")
+        bias = keep.tile([P, BLOCKS], F32, name="bias")
         warm = keep.tile([P, 1], F32, name="warm")
-        w_raw = [[keep.tile([P, PACK, HALF], F32, name=f"wr{h}{c}") for c in range(PASSES)] for h in range(2)]
-        w_bf = [[keep.tile([P, HALF, PACK], BF16, name=f"wb{h}{c}", align_bytes=64) for c in range(PASSES)] for h in range(2)]
-        w_q = [[keep.tile([P, HALF], U32, name=f"wq{h}{c}", align_bytes=64) for c in range(PASSES)] for h in range(2)]
-        w_s = [[keep.tile([P, HALF], U8, name=f"ws{h}{c}", align_bytes=64) for c in range(PASSES)] for h in range(2)]
-        x_raw = [keep.tile([P, PACK, T], F32, name=f"xr{c}") for c in range(PASSES - 1)]
-        x_last = [keep.tile([P, PACK, T // 2], F32, name=f"xl{t}") for t in range(2)]
-        x_bf = [keep.tile([P, T, PACK], BF16, name=f"xb{c}", align_bytes=64) for c in range(PASSES)]
-        x_q = [keep.tile([P, T], U32, name=f"xq{c}", align_bytes=64) for c in range(PASSES)]
-        x_s = [keep.tile([P, T], U8, name=f"xs{c}", align_bytes=64) for c in range(PASSES)]
-        g_sb = [[keep.tile([P, 2, 2, V], F32, name=f"g{h}{dd}") for dd in range(2)] for h in range(2)]
-        y = [keep.tile([P, T], F32, name=f"y{m}") for m in range(4)]
-        prod = [[keep.tile([P, 2, V], F32, name=f"pr{h}{d}") for d in range(D)] for h in range(2)]
-        part = [[keep.tile([P, 2, V], F32, name=f"pa{h}{i}") for i in range(2)] for h in range(2)]
-        res = [[keep.tile([P, V], F32, name=f"res{h}{e}") for e in range(2)] for h in range(2)]
+        w_raw, w_codes, w_scales = [], [], []
+        for g, (m0, m1) in enumerate(W_COLS):
+            w_raw.append([keep.tile([P, PACK, m1 - m0], F32, name=f"w_raw{g}{c}") for c in range(PASSES)])
+            w_codes.append(keep.tile([P, PASSES, m1 - m0], U32, name=f"w_codes{g}", align_bytes=64))
+            w_scales.append(keep.tile([P, PASSES, m1 - m0], U8, name=f"w_scales{g}", align_bytes=64))
+        x_raw = [keep.tile([P, PACK, T], F32, name=f"x_raw{c}") for c in range(LAST)]
+        x_last = [keep.tile([P, PACK, n1 - n0], F32, name=f"x_last{n0}") for n0, cut, n1 in LAST_LOADS]
+        x_bf = [keep.tile([P, T, PACK], BF16, name=f"x_bf{c}", align_bytes=64) for c in range(PASSES)]
+        x_codes = [keep.tile([P, T], U32, name=f"x_codes{c}", align_bytes=64) for c in range(PASSES)]
+        x_scales = [keep.tile([P, T], U8, name=f"x_scales{c}", align_bytes=64) for c in range(PASSES)]
+        gates = [keep.tile([P, D, V], F32, name=f"gates{m}") for m in range(BLOCKS)]
+        y = [keep.tile([P, T], F32, name=f"y{m}") for m in range(BLOCKS)]
+        total = [keep.tile([P, V], F32, name=f"total{m}") for m in range(BLOCKS)]
+        bias_bank = psum.tile([P, P], F32, name="bias_bank")
+        banks = [[psum.tile([P, n1 - n0], F32, name=f"bank{m}{n0}") for n0, n1 in RANGES[m]] for m in range(BLOCKS)]
 
-        nc.scalar.dma_start(out=bias[:], in_=b.rearrange("(h p e) o -> p h (e o)", h=2, e=2))
+        def load_w(g, c0, c1):
+            m0, m1 = W_COLS[g]
+            for c in range(c0, c1):
+                src = w[c * K_PASS : (c + 1) * K_PASS, m0:m1]
+                nc.sync.dma_start(out=w_raw[g][c][:], in_=src.rearrange("(p j) m -> p j m", j=PACK))
 
-        def load_w(h):
-            for c in range(PASSES):
-                src = w[c * K_PASS : (c + 1) * K_PASS, h * HALF : (h + 1) * HALF]
-                nc.sync.dma_start(out=w_raw[h][c][:], in_=src.rearrange("(p j) n -> p j n", j=PACK))
+        def load_gate(m):
+            src = gate[:, m * P : (m + 1) * P, :]
+            nc.sync.dma_start(out=gates[m][:], in_=src.rearrange("d p v -> p d v"))
 
-        def load_g(h):
-            for dd in range(2):
-                src = gate[2 * dd : 2 * dd + 2, h * HALF : (h + 1) * HALF, :]
-                nc.sync.dma_start(
-                    out=g_sb[h][dd][:].rearrange("p d e v -> p d (e v)"),
-                    in_=src.rearrange("d (p e) v -> p d (e v)", e=2),
-                )
+        nc.gpsimd.memset(bias_rows[:], 0.0)
+        nc.scalar.dma_start(out=bias_rows[:BLOCKS, :], in_=b.rearrange("(m p) o -> m (p o)", p=P))
+        make_identity(nc, ident[:])
 
-        load_w(0)
-        for c in range(PASSES - 1):
+        load_w(0, 0, PASSES)
+        for c in range(LAST):
             src = xT[c * K_PASS : (c + 1) * K_PASS, :]
             nc.sync.dma_start(out=x_raw[c][:], in_=src.rearrange("(p j) n -> p j n", j=PACK))
             if c == 1:
-                for d in range(D):
-                    nc.sync.dma_start(offs[d][:], lists[d])
-        for t in range(2):
-            src = xT[(PASSES - 1) * K_PASS :, t * (T // 2) : (t + 1) * (T // 2)]
-            nc.sync.dma_start(out=x_last[t][:], in_=src.rearrange("(p j) n -> p j n", j=PACK))
-        load_g(0)
-        load_w(1)
-        load_g(1)
+                for tile, pos in zip(offs, (pos1, pos2, pos3, pos4)):
+                    nc.sync.dma_start(tile[:], pos)
+        for tile, (n0, cut, n1) in zip(x_last, LAST_LOADS):
+            src = xT[LAST * K_PASS :, n0:n1]
+            nc.sync.dma_start(out=tile[:], in_=src.rearrange("(p j) n -> p j n", j=PACK))
+        load_w(1, 0, 2)
+        load_gate(0)
+        load_w(1, 2, PASSES)
+        load_gate(1)
+        load_w(2, 0, PASSES)
+        load_gate(2)
+        load_gate(3)
 
-        def interleave_w(h, c):
-            s_copy(
-                w_bf[h][c][:].rearrange("p (e m) j -> p e m j", e=2),
-                w_raw[h][c][:].rearrange("p j (m e) -> p e m j", e=2),
+        def interleave(copy, dst, src):
+            copy(
+                out=dst.rearrange("p (n i) j -> p n j i", i=4),
+                in_=src.rearrange("p j (n i) -> p n j i", i=4),
             )
 
-        def quantise_w(h, c):
+        def quantise_x(c, n0, n1):
             nc.vector.quantize_mx(
-                out=w_q[h][c][:].bitcast(FP8X4),
-                scales=w_s[h][c][:],
-                in_=w_bf[h][c][:].rearrange("p n j -> p (n j)"),
+                out=x_codes[c][:, n0:n1].bitcast(FP8X4),
+                scales=x_scales[c][:, n0:n1],
+                in_=x_bf[c][:, n0:n1, :].rearrange("p n j -> p (n j)"),
             )
 
-        def quantise_x(c, a, z):
+        def prepare_w(copy, g, c0, c1, pool, tag):
+            m0, m1 = W_COLS[g]
+            grouped = pool.tile([P, c1 - c0, m1 - m0, PACK], BF16, name=f"w_bf{g}{c0}", tag=tag, align_bytes=64)
+            for c in range(c0, c1):
+                interleave(copy, grouped[:, c - c0, :, :], w_raw[g][c][:])
             nc.vector.quantize_mx(
-                out=x_q[c][:, a:z].bitcast(FP8X4),
-                scales=x_s[c][:, a:z],
-                in_=x_bf[c][:, a:z, :].rearrange("p n j -> p (n j)"),
+                out=w_codes[g][:, c0:c1, :].rearrange("p c m -> p (c m)").bitcast(FP8X4),
+                scales=w_scales[g][:, c0:c1, :].rearrange("p c m -> p (c m)"),
+                in_=grouped[:].rearrange("p c m j -> p (c m j)"),
             )
 
-        def multiply(bank, h, e, c, a, z):
-            cols = slice(e * P, (e + 1) * P)
+        def multiply(m, c, i):
+            g = GROUP[m]
+            first = m * P - W_COLS[g][0]
+            n0, n1 = RANGES[m][i]
             nc.tensor.matmul_mx(
-                out=bank[:],
-                lhsT=w_q[h][c][:, cols].bitcast(FP8X4),
-                lhsT_scale=w_s[h][c][:, cols],
-                rhs=x_q[c][:, a:z].bitcast(FP8X4),
-                rhs_scale=x_s[c][:, a:z],
+                out=banks[m][i][:],
+                lhsT=w_codes[g][:, c, first : first + P].bitcast(FP8X4),
+                lhsT_scale=w_scales[g][:, c, first : first + P],
+                rhs=x_codes[c][:, n0:n1].bitcast(FP8X4),
+                rhs_scale=x_scales[c][:, n0:n1],
                 start=(c == 0),
-                stop=(c == PASSES - 1),
+                stop=(c == LAST),
             )
 
-        def activate(bank, h, e, a, z):
+        def activate(m, i):
+            n0, n1 = RANGES[m][i]
             nc.scalar.activation(
-                out=y[2 * h + e][:, a:z], in_=bank[:], func=RELU, bias=bias[:, h, e : e + 1], scale=1.0
+                out=y[m][:, n0:n1], in_=banks[m][i][:], func=RELU, bias=bias[:, m : m + 1], scale=1.0
             )
 
-        def gather(h, d, e):
-            nc.vector.tensor_tensor(
-                prod[h][d][:, e, :],
-                y[2 * h + e][:].indirect(offs[d][:]),
-                g_sb[h][d // 2][:, d % 2, e, :],
-                MULT,
-            )
+        def later_blocks(copy, blocks, c0, c1, tag):
+            prepare_w(copy, GROUP[blocks[0]], c0, c1, turns, tag)
+            for m in blocks:
+                for c in range(c0, c1):
+                    multiply(m, c, 0)
+                if c1 == PASSES:
+                    activate(m, 0)
+
+        def gather(m, d, dst):
+            nc.vector.tensor_tensor(dst, y[m][:].indirect(offs[d][:]), gates[m][:, d, :], MULT)
 
         def add(dst, one, two):
             nc.vector.tensor_tensor(dst, one, two, ADD)
 
-        def finish(h, e):
-            add(res[h][e][:], part[h][1][:, e, :], prod[h][3][:, e, :])
-            dst = out[h * HALF : (h + 1) * HALF, :].rearrange("(p e) v -> p e v", e=2)
-            nc.sync.dma_start(out=dst[:, e, :], in_=res[h][e][:])
-
-        def second_half(c):
-            interleave_w(1, c)
-            quantise_w(1, c)
-            for e in range(2):
-                multiply(banks1[e], 1, e, c, 0, T)
+        def store(m):
+            nc.sync.dma_start(out=out[m * P : (m + 1) * P, :], in_=total[m][:])
 
         nc.vector.memset(warm[:], 0.0)
         nc.scalar.activation(out=warm[:], in_=warm[:], func=RELU)
+        nc.tensor.transpose(bias_bank[:], bias_rows[:], ident[:])
+        nc.scalar.copy(out=bias[:], in_=bias_bank[:, :BLOCKS])
 
-        banks0 = [[psum.tile([P, T // 2], F32, name=f"b0{e}{t}") for t in range(2)] for e in range(2)]
-        banks1 = [psum.tile([P, T], F32, name=f"b1{e}") for e in range(2)]
-
-        for c in range(PASSES):
-            interleave_w(0, c)
-            quantise_w(0, c)
-        for c in range(PASSES - 1):
-            interleave(v_copy, x_bf[c][:, :V_NODES, :], x_raw[c][:, :, :V_NODES])
-            interleave(s_copy, x_bf[c][:, V_NODES:, :], x_raw[c][:, :, V_NODES:])
+        prepare_w(nc.scalar.copy, 0, 0, 2, keep, "w_bf00")
+        prepare_w(nc.scalar.copy, 0, 2, PASSES, keep, "w_bf02")
+        for c in range(LAST):
+            interleave(nc.vector.tensor_copy, x_bf[c][:, :V_NODES, :], x_raw[c][:, :, :V_NODES])
+            interleave(nc.scalar.copy, x_bf[c][:, V_NODES:, :], x_raw[c][:, :, V_NODES:])
             quantise_x(c, 0, T)
-            for e in range(2):
-                for t in range(2):
-                    multiply(banks0[e][t], 0, e, c, t * (T // 2), (t + 1) * (T // 2))
-        for t in range(2):
-            a, z = t * (T // 2), (t + 1) * (T // 2)
-            cut = 160
-            interleave(v_copy, x_bf[PASSES - 1][:, a : a + cut, :], x_last[t][:, :, :cut])
-            interleave(s_copy, x_bf[PASSES - 1][:, a + cut : z, :], x_last[t][:, :, cut:])
-            quantise_x(PASSES - 1, a, z)
-            for e in range(2):
-                multiply(banks0[e][t], 0, e, PASSES - 1, a, z)
-            for e in range(2):
-                activate(banks0[e][t], 0, e, a, z)
+            for i in range(len(RANGES[0])):
+                multiply(0, c, i)
+        for tile, (n0, cut, n1) in zip(x_last, LAST_LOADS):
+            interleave(nc.vector.tensor_copy, x_bf[LAST][:, n0:cut, :], tile[:, :, : cut - n0])
+            interleave(nc.scalar.copy, x_bf[LAST][:, cut:n1, :], tile[:, :, cut - n0 :])
+            for i, (r0, r1) in enumerate(RANGES[0]):
+                if n0 <= r0 < n1:
+                    quantise_x(LAST, r0, r1)
+                    multiply(0, LAST, i)
+                    activate(0, i)
 
-        def aggregate(h, between):
-            for d in range(D):
-                gather(h, d, 0)
-                if d == 2:
-                    add(part[h][0][:], prod[h][0][:], prod[h][1][:])
-                if d == 3:
-                    add(part[h][1][:], part[h][0][:], prod[h][2][:])
-                between(d)
-                gather(h, d, 1)
-            for e in range(2):
-                finish(h, e)
+        def product(name, count, pool, tag):
+            return pool.tile([P, count, V], F32, name=name, tag=tag, align_bytes=64)
 
-        aggregate(0, lambda d: second_half(d - 2) if d >= 2 else None)
-        second_half(2)
-        second_half(3)
-        for e in range(2):
-            activate(banks1[e], 1, e, 0, T)
-        aggregate(1, lambda d: None)
+        later_blocks(nc.vector.tensor_copy, (1,), 0, 2, "a")
+        first = product("first0", 2, keep, "first0")
+        gather(0, 0, first[:, 0, :])
+        gather(0, 1, first[:, 1, :])
+        later_blocks(nc.scalar.copy, (1,), 2, PASSES, "b")
+        second = product("second0", 2, turns, "b")
+        gather(0, 2, second[:, 0, :])
+        gather(0, 3, second[:, 1, :])
+        pairs = product("pairs0", 2, turns, "a")
+        add(pairs[:], first[:], second[:])
+
+        first = product("first1", 2, keep, "first1")
+        gather(1, 0, first[:, 0, :])
+        add(total[0][:], pairs[:, 0, :], pairs[:, 1, :])
+        store(0)
+        gather(1, 1, first[:, 1, :])
+        later_blocks(nc.scalar.copy, (2, 3), 0, 2, "c")
+        third = product("third1", 1, turns, "c")
+        gather(1, 2, third[:, 0, :])
+        later_blocks(nc.scalar.copy, (2, 3), 2, LAST, "d")
+        later_blocks(nc.scalar.copy, (2, 3), LAST, PASSES, "e")
+        fourth = product("fourth1", 1, turns, "e")
+        gather(1, 3, fourth[:, 0, :])
+        pairs = product("pairs1", 2, turns, "d")
+        add(pairs[:, 0, :], first[:, 0, :], first[:, 1, :])
+        add(pairs[:, 1, :], third[:, 0, :], fourth[:, 0, :])
+
+        products = product("products2", D, keep, "products2")
+        sums = product("sums2", 2, keep, "sums2")
+        gather(2, 0, products[:, 0, :])
+        add(total[1][:], pairs[:, 0, :], pairs[:, 1, :])
+        store(1)
+        for d in range(1, D):
+            gather(2, d, products[:, d, :])
+        last_products = product("products3", D, keep, "products3")
+        last_sums = product("sums3", 2, keep, "sums3")
+        gather(3, 0, last_products[:, 0, :])
+        add(sums[:], products[:, 0:2, :], products[:, 2:4, :])
+        gather(3, 1, last_products[:, 1, :])
+        add(total[2][:], sums[:, 0, :], sums[:, 1, :])
+        store(2)
+        gather(3, 2, last_products[:, 2, :])
+        add(last_sums[:, 0, :], last_products[:, 0, :], last_products[:, 1, :])
+        gather(3, 3, last_products[:, 3, :])
+        add(last_sums[:, 1, :], last_sums[:, 0, :], last_products[:, 2, :])
+        add(total[3][:], last_sums[:, 1, :], last_products[:, 3, :])
+        store(3)

from contextlib import ExitStack

import concourse.mybir as mybir
from concourse.masks import make_identity

K, T, D, V, N = 2048, 512, 4, 256, 512
FLOPS = 2 * K * T * N + 2 * D * N * V

F32 = mybir.dt.float32
BF16 = mybir.dt.bfloat16
U32 = mybir.dt.uint32
U16 = mybir.dt.uint16
U8 = mybir.dt.uint8
FP8X4 = mybir.dt.float8_e4m3fn_x4
ADD, MULT = mybir.AluOpType.add, mybir.AluOpType.mult
RELU = mybir.ActivationFunctionType.Relu

P = 128
PACK = 4
K_PASS = P * PACK
PASSES = K // K_PASS
LAST = PASSES - 1
BLOCKS = N // P
W_COLS = ((0, P), (P, 2 * P), (2 * P, N))
GROUP = (0, 1, 2, 2)

RANGES = (((0, 256), (256, 384), (384, T)), ((0, T),), ((0, T),), ((0, T),))

V_NODES = 320
LAST_LOADS = ((0, 240, 384), (384, 464, T))


def tile_picked_agg_lin_relu_sub_l_kernel(
    tc, xT, w, b, gate, pos1, pos2, pos3, pos4, out
):
    nc = tc.nc

    with ExitStack() as ctx:
        keep = ctx.enter_context(tc.tile_pool(name="keep", bufs=1))
        turns = ctx.enter_context(tc.tile_pool(name="turns", bufs=1))
        psum = ctx.enter_context(tc.psum_pool(name="psum", bufs=1))

        offs = [keep.tile([P, V // 16], U16, name=f"offs{d}") for d in range(D)]
        bias_rows = keep.tile([P, P], F32, name="bias_rows")
        ident = keep.tile([P, P], F32, name="ident")
        bias = keep.tile([P, BLOCKS], F32, name="bias")
        warm = keep.tile([P, 1], F32, name="warm")
        w_raw, w_codes, w_scales = [], [], []
        for g, (m0, m1) in enumerate(W_COLS):
            w_raw.append([keep.tile([P, PACK, m1 - m0], F32, name=f"w_raw{g}{c}") for c in range(PASSES)])
            w_codes.append(keep.tile([P, PASSES, m1 - m0], U32, name=f"w_codes{g}", align_bytes=64))
            w_scales.append(keep.tile([P, PASSES, m1 - m0], U8, name=f"w_scales{g}", align_bytes=64))
        x_raw = [keep.tile([P, PACK, T], F32, name=f"x_raw{c}") for c in range(LAST)]
        x_last = [keep.tile([P, PACK, n1 - n0], F32, name=f"x_last{n0}") for n0, cut, n1 in LAST_LOADS]
        x_bf = [keep.tile([P, T, PACK], BF16, name=f"x_bf{c}", align_bytes=64) for c in range(PASSES)]
        x_codes = [keep.tile([P, T], U32, name=f"x_codes{c}", align_bytes=64) for c in range(PASSES)]
        x_scales = [keep.tile([P, T], U8, name=f"x_scales{c}", align_bytes=64) for c in range(PASSES)]
        gates = [keep.tile([P, D, V], F32, name=f"gates{m}") for m in range(BLOCKS)]
        y = [keep.tile([P, T], F32, name=f"y{m}") for m in range(BLOCKS)]
        total = [keep.tile([P, V], F32, name=f"total{m}") for m in range(BLOCKS)]
        bias_bank = psum.tile([P, P], F32, name="bias_bank")
        banks = [[psum.tile([P, n1 - n0], F32, name=f"bank{m}{n0}") for n0, n1 in RANGES[m]] for m in range(BLOCKS)]

        def load_w(g, c0, c1):
            m0, m1 = W_COLS[g]
            for c in range(c0, c1):
                src = w[c * K_PASS : (c + 1) * K_PASS, m0:m1]
                nc.sync.dma_start(out=w_raw[g][c][:], in_=src.rearrange("(p j) m -> p j m", j=PACK))

        def load_gate(m):
            src = gate[:, m * P : (m + 1) * P, :]
            nc.sync.dma_start(out=gates[m][:], in_=src.rearrange("d p v -> p d v"))

        nc.gpsimd.memset(bias_rows[:], 0.0)
        nc.scalar.dma_start(out=bias_rows[:BLOCKS, :], in_=b.rearrange("(m p) o -> m (p o)", p=P))
        make_identity(nc, ident[:])

        load_w(0, 0, PASSES)
        for c in range(LAST):
            src = xT[c * K_PASS : (c + 1) * K_PASS, :]
            nc.sync.dma_start(out=x_raw[c][:], in_=src.rearrange("(p j) n -> p j n", j=PACK))
            if c == 1:
                for tile, pos in zip(offs, (pos1, pos2, pos3, pos4)):
                    nc.sync.dma_start(tile[:], pos)
        for tile, (n0, cut, n1) in zip(x_last, LAST_LOADS):
            src = xT[LAST * K_PASS :, n0:n1]
            nc.sync.dma_start(out=tile[:], in_=src.rearrange("(p j) n -> p j n", j=PACK))
        load_w(1, 0, 2)
        load_gate(0)
        load_w(1, 2, PASSES)
        load_gate(1)
        load_w(2, 0, PASSES)
        load_gate(2)
        load_gate(3)

        def interleave(copy, dst, src):
            copy(
                out=dst.rearrange("p (n i) j -> p n j i", i=4),
                in_=src.rearrange("p j (n i) -> p n j i", i=4),
            )

        def quantise_x(c, n0, n1):
            nc.vector.quantize_mx(
                out=x_codes[c][:, n0:n1].bitcast(FP8X4),
                scales=x_scales[c][:, n0:n1],
                in_=x_bf[c][:, n0:n1, :].rearrange("p n j -> p (n j)"),
            )

        def prepare_w(copy, g, c0, c1, pool, tag):
            m0, m1 = W_COLS[g]
            grouped = pool.tile([P, c1 - c0, m1 - m0, PACK], BF16, name=f"w_bf{g}{c0}", tag=tag, align_bytes=64)
            for c in range(c0, c1):
                interleave(copy, grouped[:, c - c0, :, :], w_raw[g][c][:])
            nc.vector.quantize_mx(
                out=w_codes[g][:, c0:c1, :].rearrange("p c m -> p (c m)").bitcast(FP8X4),
                scales=w_scales[g][:, c0:c1, :].rearrange("p c m -> p (c m)"),
                in_=grouped[:].rearrange("p c m j -> p (c m j)"),
            )

        def multiply(m, c, i):
            g = GROUP[m]
            first = m * P - W_COLS[g][0]
            n0, n1 = RANGES[m][i]
            nc.tensor.matmul_mx(
                out=banks[m][i][:],
                lhsT=w_codes[g][:, c, first : first + P].bitcast(FP8X4),
                lhsT_scale=w_scales[g][:, c, first : first + P],
                rhs=x_codes[c][:, n0:n1].bitcast(FP8X4),
                rhs_scale=x_scales[c][:, n0:n1],
                start=(c == 0),
                stop=(c == LAST),
            )

        def activate(m, i):
            n0, n1 = RANGES[m][i]
            nc.scalar.activation(
                out=y[m][:, n0:n1], in_=banks[m][i][:], func=RELU, bias=bias[:, m : m + 1], scale=1.0
            )

        def later_blocks(copy, blocks, c0, c1, tag):
            prepare_w(copy, GROUP[blocks[0]], c0, c1, turns, tag)
            for m in blocks:
                for c in range(c0, c1):
                    multiply(m, c, 0)
                if c1 == PASSES:
                    activate(m, 0)

        def gather(m, d, dst):
            nc.vector.tensor_tensor(dst, y[m][:].indirect(offs[d][:]), gates[m][:, d, :], MULT)

        def add(dst, one, two):
            nc.vector.tensor_tensor(dst, one, two, ADD)

        def store(m):
            nc.sync.dma_start(out=out[m * P : (m + 1) * P, :], in_=total[m][:])

        nc.vector.memset(warm[:], 0.0)
        nc.scalar.activation(out=warm[:], in_=warm[:], func=RELU)
        nc.tensor.transpose(bias_bank[:], bias_rows[:], ident[:])
        nc.scalar.copy(out=bias[:], in_=bias_bank[:, :BLOCKS])

        prepare_w(nc.scalar.copy, 0, 0, 2, keep, "w_bf00")
        prepare_w(nc.scalar.copy, 0, 2, PASSES, keep, "w_bf02")
        for c in range(LAST):
            interleave(nc.vector.tensor_copy, x_bf[c][:, :V_NODES, :], x_raw[c][:, :, :V_NODES])
            interleave(nc.scalar.copy, x_bf[c][:, V_NODES:, :], x_raw[c][:, :, V_NODES:])
            quantise_x(c, 0, T)
            for i in range(len(RANGES[0])):
                multiply(0, c, i)
        for tile, (n0, cut, n1) in zip(x_last, LAST_LOADS):
            interleave(nc.vector.tensor_copy, x_bf[LAST][:, n0:cut, :], tile[:, :, : cut - n0])
            interleave(nc.scalar.copy, x_bf[LAST][:, cut:n1, :], tile[:, :, cut - n0 :])
            for i, (r0, r1) in enumerate(RANGES[0]):
                if n0 <= r0 < n1:
                    quantise_x(LAST, r0, r1)
                    multiply(0, LAST, i)
                    activate(0, i)

        def product(name, count, pool, tag):
            return pool.tile([P, count, V], F32, name=name, tag=tag, align_bytes=64)

        later_blocks(nc.vector.tensor_copy, (1,), 0, 2, "a")
        first = product("first0", 2, keep, "first0")
        gather(0, 0, first[:, 0, :])
        gather(0, 1, first[:, 1, :])
        later_blocks(nc.scalar.copy, (1,), 2, PASSES, "b")
        second = product("second0", 2, turns, "b")
        gather(0, 2, second[:, 0, :])
        gather(0, 3, second[:, 1, :])
        pairs = product("pairs0", 2, turns, "a")
        add(pairs[:], first[:], second[:])

        first = product("first1", 2, keep, "first1")
        gather(1, 0, first[:, 0, :])
        add(total[0][:], pairs[:, 0, :], pairs[:, 1, :])
        store(0)
        gather(1, 1, first[:, 1, :])
        later_blocks(nc.scalar.copy, (2, 3), 0, 2, "c")
        third = product("third1", 1, turns, "c")
        gather(1, 2, third[:, 0, :])
        later_blocks(nc.scalar.copy, (2, 3), 2, LAST, "d")
        later_blocks(nc.scalar.copy, (2, 3), LAST, PASSES, "e")
        fourth = product("fourth1", 1, turns, "e")
        gather(1, 3, fourth[:, 0, :])
        pairs = product("pairs1", 2, turns, "d")
        add(pairs[:, 0, :], first[:, 0, :], first[:, 1, :])
        add(pairs[:, 1, :], third[:, 0, :], fourth[:, 0, :])

        products = product("products2", D, keep, "products2")
        sums = product("sums2", 2, keep, "sums2")
        gather(2, 0, products[:, 0, :])
        add(total[1][:], pairs[:, 0, :], pairs[:, 1, :])
        store(1)
        for d in range(1, D):
            gather(2, d, products[:, d, :])
        last_products = product("products3", D, keep, "products3")
        last_sums = product("sums3", 2, keep, "sums3")
        gather(3, 0, last_products[:, 0, :])
        add(sums[:], products[:, 0:2, :], products[:, 2:4, :])
        gather(3, 1, last_products[:, 1, :])
        add(total[2][:], sums[:, 0, :], sums[:, 1, :])
        store(2)
        gather(3, 2, last_products[:, 2, :])
        add(last_sums[:, 0, :], last_products[:, 0, :], last_products[:, 1, :])
        gather(3, 3, last_products[:, 3, :])
        add(last_sums[:, 1, :], last_sums[:, 0, :], last_products[:, 2, :])
        add(total[3][:], last_sums[:, 1, :], last_products[:, 3, :])
        store(3)
